import numpy as np
import ml_dtypes


def mxq(x, axis, fmt="e4m3"):
    dtype, down = {"e4m3": (ml_dtypes.float8_e4m3fn, 7), "e5m2": (ml_dtypes.float8_e5m2, 14)}[fmt]
    v = np.moveaxis(np.asarray(x, np.float32).astype(ml_dtypes.bfloat16).astype(np.float64), axis, -1)
    blocks = v.reshape(v.shape[:-1] + (-1, 32))
    amax = np.abs(blocks).max(-1, keepdims=True)
    byte = np.maximum(np.where(amax > 0, np.frexp(amax)[1] - 1 + 127, 0) - down, 1)
    scale = np.exp2(byte - 127.0)
    codes = (blocks / scale).astype(np.float32).astype(dtype).astype(np.float64)
    return np.moveaxis((codes * scale).reshape(v.shape), -1, axis)


WIDE = False


def mx_kscale(k):
    if not WIDE:
        return np.ones(k)
    levels = np.array([10, -10, 5, -5, 0])
    if k % 512:
        return np.exp2(np.random.permutation(np.resize(levels, k // 32))).repeat(32)
    a = np.empty((k // 512, 16))
    for p in range(k // 512):
        a[p, :8] = np.random.permutation(np.resize(levels, 8))
        for g in range(8):
            far = levels[np.abs(levels - a[p, g]) >= 10]
            a[p, g + 8] = far[np.random.randint(len(far))]
    return np.exp2(a.ravel()).repeat(32)


def f64(x):
    return np.asarray(x).astype(np.float64)


def striped(idx):
    return np.tile(idx.reshape(-1, 16).T, (8, 1)).astype(np.uint16)


def unstriped(offs):
    return offs[:16].T.reshape(-1).astype(np.int64)


E2M1 = np.array([0.0, 0.5, 1.0, 1.5, 2.0, 3.0, 4.0, 6.0, -0.0, -0.5, -1.0, -1.5, -2.0, -3.0, -4.0, -6.0])


def pack_weight(w, fmt):
    k, n = w.shape
    w = f64(np.asarray(w, np.float32).astype(ml_dtypes.bfloat16)).reshape(k // 32, 32, n)
    amax = np.abs(w).max(1)
    if fmt == "e4m3":
        byte = np.frexp(amax)[1] - 1 + 127 - 7
    else:
        mant, ex = np.frexp(amax / 6.0)
        byte = np.where(mant > 0.5, ex, ex - 1) + 127
    byte = np.clip(np.where(amax > 0, byte, 1), 1, 254)
    scaled = (w * np.exp2(127.0 - byte)[:, None, :]).reshape(k, n).astype(np.float32)
    by_word = np.ascontiguousarray(scaled.reshape(k // 512, 128, 4, n).transpose(0, 1, 3, 2))
    if fmt == "e4m3":
        words = by_word.astype(ml_dtypes.float8_e4m3fn).view(np.uint8)
    else:
        c = by_word.astype(ml_dtypes.float4_e2m1fn).view(np.uint8) & 0xF
        words = (c[..., 0::2] | (c[..., 1::2] << 4)).reshape(k // 512, 128, 2 * n)
    return np.ascontiguousarray(words), np.ascontiguousarray(byte.astype(np.uint8).reshape(k // 512, 16, n))


def unpack_weight(words, scales, fmt):
    g, _, n = scales.shape
    words = np.ascontiguousarray(words).reshape(g, 128, n, -1)
    if fmt == "e4m3":
        vals = words.view(ml_dtypes.float8_e4m3fn).astype(np.float64)
    else:
        nib = np.empty((g, 128, n, 4), np.uint8)
        nib[..., 0::2] = words & 0xF
        nib[..., 1::2] = words >> 4
        vals = E2M1[nib]
    vals = vals * np.repeat(np.exp2(scales.astype(np.float64) - 127.0), 8, axis=1)[..., None]
    return vals.transpose(0, 1, 3, 2).reshape(g * 512, n)


def gelu(v):
    return 0.5 * v * (1.0 + np.tanh(np.sqrt(2.0 / np.pi) * (v + 0.044715 * v**3)))


K, H, T, S, T3, S2 = 1536, 1024, 2048, 512, 1024, 512

def setup_inputs():
    n = np.random.standard_normal
    s = mx_kscale(K)[:, None]
    u = mx_kscale(H)[:, None]
    tab_words, tab_scales = pack_weight(n((K, T)) * s, "e4m3")
    tab2_words, tab2_scales = pack_weight(1.5 * n((H, T3)) / np.sqrt(H) / u, "e4m3")
    tab3_words, tab3_scales = pack_weight(n((H, T3)) / np.sqrt(H) / u, "e4m3")
    w4_words, w4_scales = pack_weight(1.3 * n((K, H)) / np.sqrt(K) / s, "e2m1")
    return {
        "tab_words": tab_words, "tab_scales": tab_scales,
        "tab2_words": tab2_words, "tab2_scales": tab2_scales,
        "tab3_words": tab3_words, "tab3_scales": tab3_scales,
        "offs": striped(np.random.permutation(T)[:S]),
        "offs2": striped(np.random.permutation(T3)[:S2]),
        "offs3": striped(np.random.permutation(T3)[:S2]),
        "w4_words": w4_words, "w4_scales": w4_scales,
        "w1": (0.55 * n((K, H)) / np.sqrt(K) / s).astype(np.float32),
        "gain": (np.exp(0.3 * n(H)) * u[:, 0]).astype(np.float32),
        "need": np.exp(0.4 * n((S2, S))).astype(np.float32),
    }

def reference(tab_words, tab_scales, tab2_words, tab2_scales, tab3_words, tab3_scales,
              offs, offs2, offs3, w4_words, w4_scales, w1, gain, need):
    v = unpack_weight(tab_words, tab_scales, "e4m3")[:, unstriped(offs)]
    v2 = unpack_weight(tab2_words, tab2_scales, "e4m3")[:, unstriped(offs2)]
    v3 = unpack_weight(tab3_words, tab3_scales, "e4m3")[:, unstriped(offs3)]
    w4 = unpack_weight(w4_words, w4_scales, "e2m1")
    w1q = mxq(f64(w1), 0, "e4m3")
    bent = np.tanh(w4.T @ v)
    wave = np.sin(w1q.T @ v)
    h = mxq((bent + wave) * f64(gain)[:, None], 0, "e4m3")
    e2 = v2.T @ h
    e3 = v3.T @ h
    return np.tanh(e2) * f64(need) + e3

@@ -1,0 +1,283 @@
+import math
+from contextlib import ExitStack
+
+import concourse.mybir as mybir
+from concourse.masks import make_identity
+
+K, H, T, S, T3, S2 = 1536, 1024, 2048, 512, 1024, 512
+FLOPS = 2 * 2 * K * H * S + 2 * 2 * H * S2 * S
+
+F32 = mybir.dt.float32
+BF16 = mybir.dt.bfloat16
+I32 = mybir.dt.int32
+U32 = mybir.dt.uint32
+U16 = mybir.dt.uint16
+U8 = mybir.dt.uint8
+FP8X4 = mybir.dt.float8_e4m3fn_x4
+FP4X4 = mybir.dt.float4_e2m1fn_x4
+ACT = mybir.ActivationFunctionType
+ALU = mybir.AluOpType
+
+P = 128
+PACK = 4
+PASS = P * PACK
+K_PASSES = K // PASS
+H_PASSES = H // PASS
+J_TILES = S // P
+M_TILES = S2 // P
+SCALAR_COLS = [512,512,0,0,0,0]
+
+
+def tile_list_berth_filling_score_kernel(
+    tc, tab_words, tab_scales, tab2_words, tab2_scales, tab3_words, tab3_scales,
+    offs, offs2, offs3, w4_words, w4_scales, w1, gain, need, out,
+):
+    nc = tc.nc
+    with ExitStack() as ctx:
+        keep = ctx.enter_context(tc.tile_pool(name="keep", bufs=1))
+        ring = ctx.enter_context(tc.tile_pool(name="ring", bufs=4))
+        stream = ctx.enter_context(tc.tile_pool(name="stream", bufs=12))
+        psum = ctx.enter_context(tc.psum_pool(name="psum", bufs=1))
+
+        def held(shape, dtype, name, tag=""):
+            return keep.tile(shape, dtype, name=name, tag=tag or name, align_bytes=64)
+
+        def streamed(shape, dtype, name):
+            return stream.tile(shape, dtype, name=name, tag="stream", align_bytes=64)
+
+        def bank(index, shape):
+            return psum.tile(shape, F32, name="bank%d" % index, tag="bank%d" % index)
+
+        def load_list(source, name):
+            offsets = keep.tile([P, S // 16], U16, name=name)
+            nc.sync.dma_start(offsets[:], source)
+            return offsets
+
+        def load_words(words, first, passes, name):
+            window = streamed([P, passes, words.shape[2]], I32, name)
+            nc.sync.dma_start(
+                window[:], words[first : first + passes].rearrange("a p c i -> p a (c i)").bitcast(I32)
+            )
+            return window
+
+        def load_scale_rows(scales, name, queue):
+            passes, rows, columns = scales.shape
+            window = held([P, columns], U8, name)
+            nc.vector.memset(window[:].bitcast(I32), 0)
+            queue.dma_start(
+                window[: rows * passes, :].bitcast(I32), scales.bitcast(I32).rearrange("a q c -> q a c")
+            )
+            return window
+
+        def gather_planes(window, offsets, passes, name, queue):
+            picked = held([P, S], U8, name + "_picked")
+            nc.vector.tensor_copy(picked[:], window[:].indirect(offsets[:]))
+            planes = held([P, passes, S], U8, name)
+            nc.gpsimd.memset(planes[:].bitcast(I32), 0)
+            for quad in range(4):
+                queue.dma_start(
+                    planes[32 * quad : 32 * quad + 4].bitcast(I32),
+                    picked[4 * passes * quad : 4 * passes * (quad + 1), :].bitcast(I32),
+                )
+            return planes
+
+        def gather_words(picked, window, offsets):
+            nc.vector.tensor_copy(picked, window.bitcast(U32).indirect(offsets[:]))
+
+        def load_w1(half, a):
+            raw = streamed([P, PACK, PASS], F32, "w1_raw%d%d" % (half, a))
+            rows = w1[a * PASS : (a + 1) * PASS, half * PASS : (half + 1) * PASS]
+            nc.sync.dma_start(raw[:], rows.rearrange("(p i) r -> p i r", i=PACK))
+            w1_raw[half, a] = raw
+
+        def quantize_w1(half, a):
+            step = half * K_PASSES + a
+            raw = w1_raw[half, a]
+            woven = held([P, PASS, PACK], BF16, "w1_woven%d" % step, "woven%d" % (step % 2))
+            split = SCALAR_COLS[step]
+            if split > 0:
+                nc.scalar.copy(
+                    woven[:, :split, :].rearrange("p (c n) i -> p c i n", n=4),
+                    raw[:, :, :split].rearrange("p i (c n) -> p c i n", n=4),
+                )
+            if split < PASS:
+                nc.vector.tensor_copy(
+                    woven[:, split:, :].rearrange("p (c n) i -> p c i n", n=4),
+                    raw[:, :, split:].rearrange("p i (c n) -> p c i n", n=4),
+                )
+            codes = held([P, PASS], U32, "w1_codes%d" % step)
+            scales = held([P, PASS], U8, "w1_scales%d" % step)
+            nc.vector.quantize_mx(
+                out=codes[:].bitcast(FP8X4), scales=scales[:], in_=woven[:].rearrange("p r i -> p (r i)")
+            )
+            w1_quant[half, a] = (codes, scales)
+
+        def w4_pass(acc, half, jt, a):
+            cols = slice(jt * P, (jt + 1) * P)
+            nc.tensor.matmul_mx(
+                out=acc[:],
+                lhsT=v_words[a][:, cols].bitcast(FP8X4), lhsT_scale=v_planes[:, a, cols],
+                rhs=w4_codes[:, a, 2 * half * PASS : 2 * (half + 1) * PASS].bitcast(FP4X4),
+                rhs_scale=w4_planes[:, a, half * PASS : (half + 1) * PASS],
+                start=(a == 0), stop=(a == K_PASSES - 1),
+            )
+
+        def w1_pass(acc, half, jt, a):
+            cols = slice(jt * P, (jt + 1) * P)
+            codes, scales = w1_quant[half, a]
+            nc.tensor.matmul_mx(
+                out=acc[:],
+                lhsT=v_words[a][:, cols].bitcast(FP8X4), lhsT_scale=v_planes[:, a, cols],
+                rhs=codes[:].bitcast(FP8X4), rhs_scale=scales[:],
+                start=(a == 0), stop=(a == K_PASSES - 1),
+            )
+
+        def minus_tanh(acc, half, jt):
+            result = held([P, PACK, P], F32, "neg_bent%d%d" % (half, jt))
+            nc.scalar.activation(result[:], acc[:].rearrange("j (q i) -> j i q", i=PACK), ACT.Tanh, scale=-1.0)
+            neg_bent[half, jt] = result
+
+        def one_minus_sin(acc, half, jt):
+            sine = ring.tile([P, PACK, P], F32, name="sine")
+            nc.scalar.activation(
+                sine[:], acc[:].rearrange("j (q i) -> j i q", i=PACK), ACT.Sin, scale=0.5, bias=minus_quarter_pi[:]
+            )
+            square = held([P, PACK, P], F32, "square%d%d" % (half, jt))
+            nc.scalar.activation(square[:], sine[:], ACT.Square, scale=math.sqrt(2.0))
+            squares[half, jt] = square
+
+        def finish_h(half, jt):
+            total = bank(jt, [P, PACK, P])
+            for term in (neg_bent[half, jt], squares[half, jt]):
+                for i in range(PACK):
+                    nc.tensor.matmul(
+                        total[:, i, :], lhsT=term[:, i, :], rhs=identity[:], is_transpose=True,
+                        start=(term is neg_bent[half, jt] and i == 0),
+                        stop=(term is squares[half, jt] and i == PACK - 1),
+                    )
+            woven = ring.tile([P, P, PACK], BF16, name="h_woven", align_bytes=64)
+            nc.vector.scalar_tensor_tensor(
+                woven[:], total[:].rearrange("p i j -> p j i"), 1.0,
+                neg_gain[:, half, :].unsqueeze(1).to_broadcast([P, P, PACK]),
+                ALU.subtract, ALU.mult,
+            )
+            codes = held([P, P], U32, "h_codes%d%d" % (half, jt))
+            scales = held([P, P], U8, "h_scales%d%d" % (half, jt))
+            nc.vector.quantize_mx(
+                out=codes[:].bitcast(FP8X4), scales=scales[:], in_=woven[:].rearrange("p j i -> p (j i)")
+            )
+            h_quant[half, jt] = (codes, scales)
+
+        def scores(acc, words, planes, jt):
+            for a in range(H_PASSES):
+                codes, scales = h_quant[a, jt]
+                for mt in range(M_TILES):
+                    cols = slice(mt * P, (mt + 1) * P)
+                    nc.tensor.matmul_mx(
+                        out=acc[:, mt, :],
+                        lhsT=words[:, a, cols].bitcast(FP8X4), lhsT_scale=planes[:, a, cols],
+                        rhs=codes[:].bitcast(FP8X4), rhs_scale=scales[:],
+                        start=(a == 0 and mt == 0), stop=(a == H_PASSES - 1 and mt == M_TILES - 1),
+                    )
+
+        def load_w4_planes():
+            planes = held([P, K_PASSES, H], U8, "w4_planes")
+            nc.vector.memset(planes[:].bitcast(I32), 0)
+            for quad in range(4):
+                nc.sync.dma_start(
+                    planes[32 * quad : 32 * quad + 4].bitcast(I32),
+                    w4_scales.bitcast(I32)[:, 4 * quad : 4 * quad + 4, :].rearrange("a r c -> r a c"),
+                )
+            return planes
+
+        w1_raw, w1_quant, neg_bent, squares, h_quant, tab_w = {}, {}, {}, {}, {}, {}
+        list1 = load_list(offs, "list1")
+        tab_s = load_scale_rows(tab_scales, "tab_s", nc.sync)
+        tab_w[0] = load_words(tab_words, 0, 1, "tab_w0")
+        w4_codes = held([P, K_PASSES, 2 * H], U8, "w4_codes")
+        nc.sync.dma_start(w4_codes[:].bitcast(I32), w4_words.bitcast(I32).rearrange("a p c -> p a c"))
+        w4_planes = load_w4_planes()
+        load_w1(0, 0)
+        tab_w[1] = load_words(tab_words, 1, 1, "tab_w1")
+        v_planes = gather_planes(tab_s, list1, K_PASSES, "v_planes", nc.sync)
+        load_w1(0, 1)
+        list2 = load_list(offs2, "list2")
+        tab2_s = load_scale_rows(tab2_scales, "tab2_s", nc.sync)
+        tab_w[2] = load_words(tab_words, 2, 1, "tab_w2")
+        list3 = load_list(offs3, "list3")
+        tab3_s = load_scale_rows(tab3_scales, "tab3_s", nc.sync)
+        load_w1(0, 2)
+        gain_tile = keep.tile([P, H_PASSES, PACK], F32, name="gain_tile")
+        nc.sync.dma_start(gain_tile[:], gain.rearrange("(a p i) -> p a i", a=H_PASSES, i=PACK))
+        v_words = {}
+        for a in range(K_PASSES):
+            v_words[a] = held([P, S], U32, "v_words%d" % a)
+            gather_words(v_words[a][:], tab_w[a][:, 0, :], list1)
+        v2_planes = gather_planes(tab2_s, list2, H_PASSES, "v2_planes", nc.sync)
+        load_w1(1, 0)
+        v3_planes = gather_planes(tab3_s, list3, H_PASSES, "v3_planes", nc.sync)
+        load_w1(1, 1)
+        load_w1(1, 2)
+        tab2_w = load_words(tab2_words, 0, H_PASSES, "tab2_w")
+        tab3_w = load_words(tab3_words, 0, H_PASSES, "tab3_w")
+        need_tile = streamed([P, M_TILES, S], F32, "need_tile")
+        nc.sync.dma_start(need_tile[:], need.rearrange("(mt p) j -> p mt j", p=P))
+
+        identity = held([P, P], F32, "identity")
+        make_identity(nc, identity[:])
+        one = keep.tile([P, 1], F32, name="one")
+        nc.vector.memset(one[:], 1.0)
+        minus_quarter_pi = keep.tile([P, 1], F32, name="minus_quarter_pi")
+        nc.vector.tensor_scalar(minus_quarter_pi[:], one[:], -math.pi / 4, None, ALU.mult)
+        neg_gain = keep.tile([P, H_PASSES, PACK], F32, name="neg_gain")
+        nc.gpsimd.tensor_scalar(neg_gain[:], gain_tile[:], -1.0, 0.0, ALU.mult, ALU.add)
+
+        bent_acc = [bank(index, [P, PASS]) for index in range(H_PASSES * J_TILES)]
+        for a in range(K_PASSES):
+            if a < 2:
+                quantize_w1(0, a)
+            for half in range(H_PASSES):
+                for jt in range(J_TILES):
+                    w4_pass(bent_acc[half * J_TILES + jt], half, jt, a)
+        for half in range(H_PASSES):
+            for jt in range(J_TILES):
+                minus_tanh(bent_acc[half * J_TILES + jt], half, jt)
+        for a in range(2, K_PASSES):
+            quantize_w1(0, a)
+        for jt in range(J_TILES):
+            acc = bank(jt, [P, PASS])
+            for a in range(K_PASSES):
+                w1_pass(acc, 0, jt, a)
+            one_minus_sin(acc, 0, jt)
+        wave_acc = [bank(J_TILES + jt, [P, PASS]) for jt in range(J_TILES)]
+        for a in range(K_PASSES):
+            quantize_w1(1, a)
+            for jt in range(J_TILES):
+                w1_pass(wave_acc[jt], 1, jt, a)
+        for jt in range(J_TILES):
+            one_minus_sin(wave_acc[jt], 1, jt)
+        for jt in range(J_TILES):
+            finish_h(0, jt)
+        v2_words = held([P, H_PASSES, S], U32, "v2_words", "woven1")
+        for a in range(H_PASSES):
+            gather_words(v2_words[:, a, :], tab2_w[:, a, :], list2)
+        for jt in range(J_TILES):
+            finish_h(1, jt)
+        v3_words = held([P, H_PASSES, S], U32, "v3_words", "v_words2")
+        for a in range(H_PASSES):
+            gather_words(v3_words[:, a, :], tab3_w[:, a, :], list3)
+
+        out_view = out.rearrange("(mt p) j -> p mt j", p=P)
+        for jt in range(J_TILES):
+            e2 = bank(J_TILES + jt, [P, M_TILES, P])
+            e3 = bank(jt, [P, M_TILES, P])
+            scores(e2, v2_words, v2_planes, jt)
+            scores(e3, v3_words, v3_planes, jt)
+            cols = slice(jt * P, (jt + 1) * P)
+            bounded = ring.tile([P, M_TILES, P], F32, name="bounded")
+            nc.scalar.activation(bounded[:], e2[:], ACT.Tanh)
+            scaled = ring.tile([P, M_TILES, P], F32, name="scaled")
+            nc.vector.tensor_tensor(scaled[:], bounded[:], need_tile[:, :, cols], ALU.mult)
+            result = ring.tile([P, M_TILES, P], F32, name="result")
+            nc.vector.tensor_tensor(result[:], e3[:], scaled[:], ALU.add)
+            nc.sync.dma_start(out_view[:, :, cols], result[:])

@@ -229,6 +229,8 @@ def tile_list_berth_filling_score_kernel(
         nc.vector.memset(one[:], 1.0)
         minus_quarter_pi = keep.tile([P, 1], F32, name="minus_quarter_pi")
         nc.vector.tensor_scalar(minus_quarter_pi[:], one[:], -math.pi / 4, None, ALU.mult)
+        table_choice = keep.tile([P, 1], F32, name="table_choice")
+        nc.scalar.activation(table_choice[:], one[:], ACT.Silu)
         neg_gain = keep.tile([P, H_PASSES, PACK], F32, name="neg_gain")
         nc.gpsimd.tensor_scalar(neg_gain[:], gain_tile[:], -1.0, 0.0, ALU.mult, ALU.add)
 

@@ -25,7 +25,7 @@ K_PASSES = K // PASS
 H_PASSES = H // PASS
 J_TILES = S // P
 M_TILES = S2 // P
-SCALAR_COLS = [512,512,0,0,0,0]
+PAIR = 2 * P
 
 
 def tile_list_berth_filling_score_kernel(
@@ -36,14 +36,10 @@ def tile_list_berth_filling_score_kernel(
     with ExitStack() as ctx:
         keep = ctx.enter_context(tc.tile_pool(name="keep", bufs=1))
         ring = ctx.enter_context(tc.tile_pool(name="ring", bufs=4))
-        stream = ctx.enter_context(tc.tile_pool(name="stream", bufs=12))
         psum = ctx.enter_context(tc.psum_pool(name="psum", bufs=1))
 
         def held(shape, dtype, name, tag=""):
             return keep.tile(shape, dtype, name=name, tag=tag or name, align_bytes=64)
-
-        def streamed(shape, dtype, name):
-            return stream.tile(shape, dtype, name=name, tag="stream", align_bytes=64)
 
         def bank(index, shape):
             return psum.tile(shape, F32, name="bank%d" % index, tag="bank%d" % index)
@@ -54,7 +50,7 @@ def tile_list_berth_filling_score_kernel(
             return offsets
 
         def load_words(words, first, passes, name):
-            window = streamed([P, passes, words.shape[2]], I32, name)
+            window = held([P, passes, words.shape[2]], I32, name)
             nc.sync.dma_start(
                 window[:], words[first : first + passes].rearrange("a p c i -> p a (c i)").bitcast(I32)
             )
@@ -69,8 +65,8 @@ def tile_list_berth_filling_score_kernel(
             )
             return window
 
-        def gather_planes(window, offsets, passes, name, queue):
-            picked = held([P, S], U8, name + "_picked")
+        def gather_planes(window, offsets, passes, name, queue, tag=""):
+            picked = held([P, S], U8, name + "_picked", tag)
             nc.vector.tensor_copy(picked[:], window[:].indirect(offsets[:]))
             planes = held([P, passes, S], U8, name)
             nc.gpsimd.memset(planes[:].bitcast(I32), 0)
@@ -85,31 +81,34 @@ def tile_list_berth_filling_score_kernel(
             nc.vector.tensor_copy(picked, window.bitcast(U32).indirect(offsets[:]))
 
         def load_w1(half, a):
-            raw = streamed([P, PACK, PASS], F32, "w1_raw%d%d" % (half, a))
+            raw = held([P, PACK, PASS], F32, "w1_raw%d%d" % (half, a))
             rows = w1[a * PASS : (a + 1) * PASS, half * PASS : (half + 1) * PASS]
             nc.sync.dma_start(raw[:], rows.rearrange("(p i) r -> p i r", i=PACK))
             w1_raw[half, a] = raw
 
-        def quantize_w1(half, a):
-            step = half * K_PASSES + a
-            raw = w1_raw[half, a]
-            woven = held([P, PASS, PACK], BF16, "w1_woven%d" % step, "woven%d" % (step % 2))
-            split = SCALAR_COLS[step]
-            if split > 0:
-                nc.scalar.copy(
-                    woven[:, :split, :].rearrange("p (c n) i -> p c i n", n=4),
-                    raw[:, :, :split].rearrange("p i (c n) -> p c i n", n=4),
-                )
-            if split < PASS:
-                nc.vector.tensor_copy(
-                    woven[:, split:, :].rearrange("p (c n) i -> p c i n", n=4),
-                    raw[:, :, split:].rearrange("p i (c n) -> p c i n", n=4),
-                )
-            codes = held([P, PASS], U32, "w1_codes%d" % step)
-            scales = held([P, PASS], U8, "w1_scales%d" % step)
-            nc.vector.quantize_mx(
-                out=codes[:].bitcast(FP8X4), scales=scales[:], in_=woven[:].rearrange("p r i -> p (r i)")
+        def weave(engine_copy, woven, raw):
+            engine_copy(
+                woven.rearrange("p (c n) i -> p c i n", n=4), raw.rearrange("p i (c n) -> p c i n", n=4)
             )
+
+        def woven_tile(width, name, tag):
+            return held([P, width, PACK], BF16, name, tag)[:]
+
+        def quantize_w1(half, a, pieces):
+            raw = w1_raw[half, a]
+            codes = held([P, PASS], U32, "w1_codes%d%d" % (half, a), "tab_w2" if (half, a) == (0, 1) else "")
+            scales = held([P, PASS], U8, "w1_scales%d%d" % (half, a))
+            first = 0
+            for width, scalar_cols, woven in pieces:
+                if scalar_cols > 0:
+                    weave(nc.scalar.copy, woven[:, :scalar_cols, :], raw[:, :, first : first + scalar_cols])
+                if scalar_cols < width:
+                    weave(nc.vector.tensor_copy, woven[:, scalar_cols:, :], raw[:, :, first + scalar_cols : first + width])
+                nc.vector.quantize_mx(
+                    out=codes[:, first : first + width].bitcast(FP8X4), scales=scales[:, first : first + width],
+                    in_=woven.rearrange("p r i -> p (r i)"),
+                )
+                first = first + width
             w1_quant[half, a] = (codes, scales)
 
         def w4_pass(acc, half, jt, a):
@@ -133,51 +132,55 @@ def tile_list_berth_filling_score_kernel(
             )
 
         def minus_tanh(acc, half, jt):
-            result = held([P, PACK, P], F32, "neg_bent%d%d" % (half, jt))
+            result = held([P, PACK, P], F32, "neg_bent%d%d" % (half, jt), "w1_raw01" if (half, jt) == (0, 0) else "")
             nc.scalar.activation(result[:], acc[:].rearrange("j (q i) -> j i q", i=PACK), ACT.Tanh, scale=-1.0)
             neg_bent[half, jt] = result
 
         def one_minus_sin(acc, half, jt):
-            sine = ring.tile([P, PACK, P], F32, name="sine")
+            sine = held([P, PACK, P], F32, "sine%d%d" % (half, jt), "sine%d" % jt)
             nc.scalar.activation(
                 sine[:], acc[:].rearrange("j (q i) -> j i q", i=PACK), ACT.Sin, scale=0.5, bias=minus_quarter_pi[:]
             )
+            sines[half, jt] = sine
             square = held([P, PACK, P], F32, "square%d%d" % (half, jt))
             nc.scalar.activation(square[:], sine[:], ACT.Square, scale=math.sqrt(2.0))
             squares[half, jt] = square
 
-        def finish_h(half, jt):
-            total = bank(jt, [P, PACK, P])
-            for term in (neg_bent[half, jt], squares[half, jt]):
-                for i in range(PACK):
-                    nc.tensor.matmul(
-                        total[:, i, :], lhsT=term[:, i, :], rhs=identity[:], is_transpose=True,
-                        start=(term is neg_bent[half, jt] and i == 0),
-                        stop=(term is squares[half, jt] and i == PACK - 1),
-                    )
-            woven = ring.tile([P, P, PACK], BF16, name="h_woven", align_bytes=64)
-            nc.vector.scalar_tensor_tensor(
-                woven[:], total[:].rearrange("p i j -> p j i"), 1.0,
-                neg_gain[:, half, :].unsqueeze(1).to_broadcast([P, P, PACK]),
-                ALU.subtract, ALU.mult,
-            )
-            codes = held([P, P], U32, "h_codes%d%d" % (half, jt))
-            scales = held([P, P], U8, "h_scales%d%d" % (half, jt))
+        def finish_h(half, pair):
+            woven = ring.tile([P, PAIR, PACK], BF16, name="h_woven", align_bytes=64)
+            for member in range(2):
+                jt = 2 * pair + member
+                total = bank(jt, [P, PACK, P])
+                for term in (neg_bent[half, jt], squares[half, jt]):
+                    for i in range(PACK):
+                        nc.tensor.matmul(
+                            total[:, i, :], lhsT=term[:, i, :], rhs=identity[:], is_transpose=True,
+                            start=(term is neg_bent[half, jt] and i == 0),
+                            stop=(term is squares[half, jt] and i == PACK - 1),
+                        )
+                nc.vector.scalar_tensor_tensor(
+                    woven[:, member * P : (member + 1) * P, :], total[:].rearrange("p i j -> p j i"), 1.0,
+                    neg_gain[:, half, :].unsqueeze(1).to_broadcast([P, P, PACK]),
+                    ALU.subtract, ALU.mult,
+                )
+            codes = held([P, PAIR], U32, "h_codes%d%d" % (half, pair))
+            scales = held([P, PAIR], U8, "h_scales%d%d" % (half, pair))
             nc.vector.quantize_mx(
                 out=codes[:].bitcast(FP8X4), scales=scales[:], in_=woven[:].rearrange("p j i -> p (j i)")
             )
-            h_quant[half, jt] = (codes, scales)
+            h_quant[half, pair] = (codes, scales)
 
-        def scores(acc, words, planes, jt):
-            for a in range(H_PASSES):
-                codes, scales = h_quant[a, jt]
-                for mt in range(M_TILES):
-                    cols = slice(mt * P, (mt + 1) * P)
+        def scores(acc, words, planes, block, passes):
+            pair, first_mt = block // 2, 2 * (block % 2)
+            for a in passes:
+                codes, scales = h_quant[a, pair]
+                for member in range(2):
+                    cols = slice((first_mt + member) * P, (first_mt + member + 1) * P)
                     nc.tensor.matmul_mx(
-                        out=acc[:, mt, :],
+                        out=acc[:, member, :],
                         lhsT=words[:, a, cols].bitcast(FP8X4), lhsT_scale=planes[:, a, cols],
                         rhs=codes[:].bitcast(FP8X4), rhs_scale=scales[:],
-                        start=(a == 0 and mt == 0), stop=(a == H_PASSES - 1 and mt == M_TILES - 1),
+                        start=(a == 0 and member == 0), stop=(a == H_PASSES - 1 and member == 1),
                     )
 
         def load_w4_planes():
@@ -191,6 +194,7 @@ def tile_list_berth_filling_score_kernel(
             return planes
 
         w1_raw, w1_quant, neg_bent, squares, h_quant, tab_w = {}, {}, {}, {}, {}, {}
+        sines = {}
         list1 = load_list(offs, "list1")
         tab_s = load_scale_rows(tab_scales, "tab_s", nc.sync)
         tab_w[0] = load_words(tab_words, 0, 1, "tab_w0")
@@ -203,9 +207,9 @@ def tile_list_berth_filling_score_kernel(
         load_w1(0, 1)
         list2 = load_list(offs2, "list2")
         tab2_s = load_scale_rows(tab2_scales, "tab2_s", nc.sync)
-        tab_w[2] = load_words(tab_words, 2, 1, "tab_w2")
         list3 = load_list(offs3, "list3")
         tab3_s = load_scale_rows(tab3_scales, "tab3_s", nc.sync)
+        tab_w[2] = load_words(tab_words, 2, 1, "tab_w2")
         load_w1(0, 2)
         gain_tile = keep.tile([P, H_PASSES, PACK], F32, name="gain_tile")
         nc.sync.dma_start(gain_tile[:], gain.rearrange("(a p i) -> p a i", a=H_PASSES, i=PACK))
@@ -213,14 +217,23 @@ def tile_list_berth_filling_score_kernel(
         for a in range(K_PASSES):
             v_words[a] = held([P, S], U32, "v_words%d" % a)
             gather_words(v_words[a][:], tab_w[a][:, 0, :], list1)
-        v2_planes = gather_planes(tab2_s, list2, H_PASSES, "v2_planes", nc.sync)
         load_w1(1, 0)
-        v3_planes = gather_planes(tab3_s, list3, H_PASSES, "v3_planes", nc.sync)
         load_w1(1, 1)
         load_w1(1, 2)
+        crew_picked = held([P, 2, S], U8, "crew_picked")
+        nc.vector.tensor_copy(crew_picked[:, 0, :], tab2_s[:].indirect(list2[:]))
+        nc.vector.tensor_copy(crew_picked[:, 1, :], tab3_s[:].indirect(list3[:]))
+        crew_planes = held([P, H_PASSES, 2, S], U8, "crew_planes")
+        nc.gpsimd.memset(crew_planes[:].bitcast(I32), 0)
+        for quad in range(4):
+            nc.sync.dma_start(
+                crew_planes[32 * quad : 32 * quad + 4].rearrange("p a n s -> p a (n s)").bitcast(I32),
+                crew_picked[8 * quad : 8 * (quad + 1)].rearrange("p n s -> p (n s)").bitcast(I32),
+            )
+        v2_planes, v3_planes = crew_planes[:, :, 0, :], crew_planes[:, :, 1, :]
         tab2_w = load_words(tab2_words, 0, H_PASSES, "tab2_w")
         tab3_w = load_words(tab3_words, 0, H_PASSES, "tab3_w")
-        need_tile = streamed([P, M_TILES, S], F32, "need_tile")
+        need_tile = held([P, M_TILES, S], F32, "need_tile")
         nc.sync.dma_start(need_tile[:], need.rearrange("(mt p) j -> p mt j", p=P))
 
         identity = held([P, P], F32, "identity")
@@ -235,51 +248,56 @@ def tile_list_berth_filling_score_kernel(
         nc.gpsimd.tensor_scalar(neg_gain[:], gain_tile[:], -1.0, 0.0, ALU.mult, ALU.add)
 
         bent_acc = [bank(index, [P, PASS]) for index in range(H_PASSES * J_TILES)]
+        quantize_w1(0, 0, [(512, 512, woven_tile(512, "woven0", "woven_a"))])
         for a in range(K_PASSES):
-            if a < 2:
-                quantize_w1(0, a)
             for half in range(H_PASSES):
                 for jt in range(J_TILES):
                     w4_pass(bent_acc[half * J_TILES + jt], half, jt, a)
+        quantize_w1(0, 1, [(512, 512, woven_tile(512, "woven1", "woven_b"))])
         for half in range(H_PASSES):
             for jt in range(J_TILES):
                 minus_tanh(bent_acc[half * J_TILES + jt], half, jt)
-        for a in range(2, K_PASSES):
-            quantize_w1(0, a)
+        quantize_w1(0, 2, [(512, 0, woven_tile(512, "woven2", "woven_a"))])
         for jt in range(J_TILES):
             acc = bank(jt, [P, PASS])
             for a in range(K_PASSES):
                 w1_pass(acc, 0, jt, a)
             one_minus_sin(acc, 0, jt)
+        quantize_w1(1, 0, [(512, 0, woven_tile(512, "woven3", "woven_b"))])
+        quantize_w1(1, 1, [(512, 0, woven_tile(512, "woven4", "woven_a"))])
+        quantize_w1(1, 2, [(512, 0, woven_tile(512, "woven5", "woven_b"))])
         wave_acc = [bank(J_TILES + jt, [P, PASS]) for jt in range(J_TILES)]
         for a in range(K_PASSES):
-            quantize_w1(1, a)
             for jt in range(J_TILES):
                 w1_pass(wave_acc[jt], 1, jt, a)
         for jt in range(J_TILES):
             one_minus_sin(wave_acc[jt], 1, jt)
-        for jt in range(J_TILES):
-            finish_h(0, jt)
-        v2_words = held([P, H_PASSES, S], U32, "v2_words", "woven1")
+        for pair in range(J_TILES // 2):
+            finish_h(0, pair)
+        v2_words = held([P, H_PASSES, S], U32, "v2_words", "square03")
         for a in range(H_PASSES):
             gather_words(v2_words[:, a, :], tab2_w[:, a, :], list2)
-        for jt in range(J_TILES):
-            finish_h(1, jt)
         v3_words = held([P, H_PASSES, S], U32, "v3_words", "v_words2")
         for a in range(H_PASSES):
             gather_words(v3_words[:, a, :], tab3_w[:, a, :], list3)
+        e2_acc = [bank(J_TILES + block, [P, 2, PAIR]) for block in range(J_TILES)]
+        for block in range(J_TILES):
+            scores(e2_acc[block], v2_words, v2_planes, block, (0,))
+        for pair in range(J_TILES // 2):
+            finish_h(1, pair)
 
         out_view = out.rearrange("(mt p) j -> p mt j", p=P)
-        for jt in range(J_TILES):
-            e2 = bank(J_TILES + jt, [P, M_TILES, P])
-            e3 = bank(jt, [P, M_TILES, P])
-            scores(e2, v2_words, v2_planes, jt)
-            scores(e3, v3_words, v3_planes, jt)
-            cols = slice(jt * P, (jt + 1) * P)
-            bounded = ring.tile([P, M_TILES, P], F32, name="bounded")
+        for block in range(J_TILES):
+            e2 = e2_acc[block]
+            e3 = bank(block, [P, 2, PAIR])
+            scores(e2, v2_words, v2_planes, block, (1,))
+            scores(e3, v3_words, v3_planes, block, (0, 1))
+            rows = slice(2 * (block % 2), 2 * (block % 2) + 2)
+            cols = slice(block // 2 * PAIR, (block // 2 + 1) * PAIR)
+            bounded = ring.tile([P, 2, PAIR], F32, name="bounded")
             nc.scalar.activation(bounded[:], e2[:], ACT.Tanh)
-            scaled = ring.tile([P, M_TILES, P], F32, name="scaled")
-            nc.vector.tensor_tensor(scaled[:], bounded[:], need_tile[:, :, cols], ALU.mult)
-            result = ring.tile([P, M_TILES, P], F32, name="result")
+            scaled = ring.tile([P, 2, PAIR], F32, name="scaled")
+            nc.vector.tensor_tensor(scaled[:], bounded[:], need_tile[:, rows, cols], ALU.mult)
+            result = ring.tile([P, 2, PAIR], F32, name="result")
             nc.vector.tensor_tensor(result[:], e3[:], scaled[:], ALU.add)
-            nc.sync.dma_start(out_view[:, :, cols], result[:])
+            nc.sync.dma_start(out_view[:, rows, cols], result[:])

@@ -196,16 +196,16 @@ def tile_list_berth_filling_score_kernel(
         w1_raw, w1_quant, neg_bent, squares, h_quant, tab_w = {}, {}, {}, {}, {}, {}
         sines = {}
         list1 = load_list(offs, "list1")
-        tab_s = load_scale_rows(tab_scales, "tab_s", nc.sync)
         tab_w[0] = load_words(tab_words, 0, 1, "tab_w0")
+        tab_s = load_scale_rows(tab_scales, "tab_s", nc.sync)
         w4_codes = held([P, K_PASSES, 2 * H], U8, "w4_codes")
         nc.sync.dma_start(w4_codes[:].bitcast(I32), w4_words.bitcast(I32).rearrange("a p c -> p a c"))
         w4_planes = load_w4_planes()
         load_w1(0, 0)
         tab_w[1] = load_words(tab_words, 1, 1, "tab_w1")
+        list2 = load_list(offs2, "list2")
         v_planes = gather_planes(tab_s, list1, K_PASSES, "v_planes", nc.sync)
         load_w1(0, 1)
-        list2 = load_list(offs2, "list2")
         tab2_s = load_scale_rows(tab2_scales, "tab2_s", nc.sync)
         list3 = load_list(offs3, "list3")
         tab3_s = load_scale_rows(tab3_scales, "tab3_s", nc.sync)
@@ -215,7 +215,7 @@ def tile_list_berth_filling_score_kernel(
         nc.sync.dma_start(gain_tile[:], gain.rearrange("(a p i) -> p a i", a=H_PASSES, i=PACK))
         v_words = {}
         for a in range(K_PASSES):
-            v_words[a] = held([P, S], U32, "v_words%d" % a)
+            v_words[a] = held([P, S], U32, "v_words%d" % a, "tab_s" if a == 0 else "")
             gather_words(v_words[a][:], tab_w[a][:, 0, :], list1)
         load_w1(1, 0)
         load_w1(1, 1)
@@ -299,5 +299,8 @@ def tile_list_berth_filling_score_kernel(
             scaled = ring.tile([P, 2, PAIR], F32, name="scaled")
             nc.vector.tensor_tensor(scaled[:], bounded[:], need_tile[:, rows, cols], ALU.mult)
             result = ring.tile([P, 2, PAIR], F32, name="result")
-            nc.vector.tensor_tensor(result[:], e3[:], scaled[:], ALU.add)
-            nc.sync.dma_start(out_view[:, rows, cols], result[:])
+            pieces = 2 if block == J_TILES - 1 else 1
+            for piece in range(pieces):
+                part = slice(piece * 2 // pieces, (piece + 1) * 2 // pieces)
+                nc.vector.tensor_tensor(result[:, part, :], e3[:, part, :], scaled[:, part, :], ALU.add)
+                nc.sync.dma_start(out_view[:, rows, cols][:, part, :], result[:, part, :])

import math
from contextlib import ExitStack

import concourse.mybir as mybir
from concourse.masks import make_identity

K, H, T, S, T3, S2 = 1536, 1024, 2048, 512, 1024, 512
FLOPS = 2 * 2 * K * H * S + 2 * 2 * H * S2 * S

F32 = mybir.dt.float32
BF16 = mybir.dt.bfloat16
I32 = mybir.dt.int32
U32 = mybir.dt.uint32
U16 = mybir.dt.uint16
U8 = mybir.dt.uint8
FP8X4 = mybir.dt.float8_e4m3fn_x4
FP4X4 = mybir.dt.float4_e2m1fn_x4
ACT = mybir.ActivationFunctionType
ALU = mybir.AluOpType

P = 128
PACK = 4
PASS = P * PACK
K_PASSES = K // PASS
H_PASSES = H // PASS
J_TILES = S // P
M_TILES = S2 // P
PAIR = 2 * P


def tile_list_berth_filling_score_kernel(
    tc, tab_words, tab_scales, tab2_words, tab2_scales, tab3_words, tab3_scales,
    offs, offs2, offs3, w4_words, w4_scales, w1, gain, need, out,
):
    nc = tc.nc
    with ExitStack() as ctx:
        keep = ctx.enter_context(tc.tile_pool(name="keep", bufs=1))
        ring = ctx.enter_context(tc.tile_pool(name="ring", bufs=4))
        psum = ctx.enter_context(tc.psum_pool(name="psum", bufs=1))

        def held(shape, dtype, name, tag=""):
            return keep.tile(shape, dtype, name=name, tag=tag or name, align_bytes=64)

        def bank(index, shape):
            return psum.tile(shape, F32, name="bank%d" % index, tag="bank%d" % index)

        def load_list(source, name):
            offsets = keep.tile([P, S // 16], U16, name=name)
            nc.sync.dma_start(offsets[:], source)
            return offsets

        def load_words(words, first, passes, name):
            window = held([P, passes, words.shape[2]], I32, name)
            nc.sync.dma_start(
                window[:], words[first : first + passes].rearrange("a p c i -> p a (c i)").bitcast(I32)
            )
            return window

        def load_scale_rows(scales, name, queue):
            passes, rows, columns = scales.shape
            window = held([P, columns], U8, name)
            nc.vector.memset(window[:].bitcast(I32), 0)
            queue.dma_start(
                window[: rows * passes, :].bitcast(I32), scales.bitcast(I32).rearrange("a q c -> q a c")
            )
            return window

        def gather_planes(window, offsets, passes, name, queue, tag=""):
            picked = held([P, S], U8, name + "_picked", tag)
            nc.vector.tensor_copy(picked[:], window[:].indirect(offsets[:]))
            planes = held([P, passes, S], U8, name)
            nc.gpsimd.memset(planes[:].bitcast(I32), 0)
            for quad in range(4):
                queue.dma_start(
                    planes[32 * quad : 32 * quad + 4].bitcast(I32),
                    picked[4 * passes * quad : 4 * passes * (quad + 1), :].bitcast(I32),
                )
            return planes

        def gather_words(picked, window, offsets):
            nc.vector.tensor_copy(picked, window.bitcast(U32).indirect(offsets[:]))

        def load_w1(half, a):
            raw = held([P, PACK, PASS], F32, "w1_raw%d%d" % (half, a))
            rows = w1[a * PASS : (a + 1) * PASS, half * PASS : (half + 1) * PASS]
            nc.sync.dma_start(raw[:], rows.rearrange("(p i) r -> p i r", i=PACK))
            w1_raw[half, a] = raw

        def weave(engine_copy, woven, raw):
            engine_copy(
                woven.rearrange("p (c n) i -> p c i n", n=4), raw.rearrange("p i (c n) -> p c i n", n=4)
            )

        def woven_tile(width, name, tag):
            return held([P, width, PACK], BF16, name, tag)[:]

        def quantize_w1(half, a, pieces):
            raw = w1_raw[half, a]
            codes = held([P, PASS], U32, "w1_codes%d%d" % (half, a), "tab_w2" if (half, a) == (0, 1) else "")
            scales = held([P, PASS], U8, "w1_scales%d%d" % (half, a))
            first = 0
            for width, scalar_cols, woven in pieces:
                if scalar_cols > 0:
                    weave(nc.scalar.copy, woven[:, :scalar_cols, :], raw[:, :, first : first + scalar_cols])
                if scalar_cols < width:
                    weave(nc.vector.tensor_copy, woven[:, scalar_cols:, :], raw[:, :, first + scalar_cols : first + width])
                nc.vector.quantize_mx(
                    out=codes[:, first : first + width].bitcast(FP8X4), scales=scales[:, first : first + width],
                    in_=woven.rearrange("p r i -> p (r i)"),
                )
                first = first + width
            w1_quant[half, a] = (codes, scales)

        def w4_pass(acc, half, jt, a):
            cols = slice(jt * P, (jt + 1) * P)
            nc.tensor.matmul_mx(
                out=acc[:],
                lhsT=v_words[a][:, cols].bitcast(FP8X4), lhsT_scale=v_planes[:, a, cols],
                rhs=w4_codes[:, a, 2 * half * PASS : 2 * (half + 1) * PASS].bitcast(FP4X4),
                rhs_scale=w4_planes[:, a, half * PASS : (half + 1) * PASS],
                start=(a == 0), stop=(a == K_PASSES - 1),
            )

        def w1_pass(acc, half, jt, a):
            cols = slice(jt * P, (jt + 1) * P)
            codes, scales = w1_quant[half, a]
            nc.tensor.matmul_mx(
                out=acc[:],
                lhsT=v_words[a][:, cols].bitcast(FP8X4), lhsT_scale=v_planes[:, a, cols],
                rhs=codes[:].bitcast(FP8X4), rhs_scale=scales[:],
                start=(a == 0), stop=(a == K_PASSES - 1),
            )

        def minus_tanh(acc, half, jt):
            result = held([P, PACK, P], F32, "neg_bent%d%d" % (half, jt), "w1_raw01" if (half, jt) == (0, 0) else "")
            nc.scalar.activation(result[:], acc[:].rearrange("j (q i) -> j i q", i=PACK), ACT.Tanh, scale=-1.0)
            neg_bent[half, jt] = result

        def one_minus_sin(acc, half, jt):
            sine = held([P, PACK, P], F32, "sine%d%d" % (half, jt), "sine%d" % jt)
            nc.scalar.activation(
                sine[:], acc[:].rearrange("j (q i) -> j i q", i=PACK), ACT.Sin, scale=0.5, bias=minus_quarter_pi[:]
            )
            sines[half, jt] = sine
            square = held([P, PACK, P], F32, "square%d%d" % (half, jt))
            nc.scalar.activation(square[:], sine[:], ACT.Square, scale=math.sqrt(2.0))
            squares[half, jt] = square

        def finish_h(half, pair):
            woven = ring.tile([P, PAIR, PACK], BF16, name="h_woven", align_bytes=64)
            for member in range(2):
                jt = 2 * pair + member
                total = bank(jt, [P, PACK, P])
                for term in (neg_bent[half, jt], squares[half, jt]):
                    for i in range(PACK):
                        nc.tensor.matmul(
                            total[:, i, :], lhsT=term[:, i, :], rhs=identity[:], is_transpose=True,
                            start=(term is neg_bent[half, jt] and i == 0),
                            stop=(term is squares[half, jt] and i == PACK - 1),
                        )
                nc.vector.scalar_tensor_tensor(
                    woven[:, member * P : (member + 1) * P, :], total[:].rearrange("p i j -> p j i"), 1.0,
                    neg_gain[:, half, :].unsqueeze(1).to_broadcast([P, P, PACK]),
                    ALU.subtract, ALU.mult,
                )
            codes = held([P, PAIR], U32, "h_codes%d%d" % (half, pair))
            scales = held([P, PAIR], U8, "h_scales%d%d" % (half, pair))
            nc.vector.quantize_mx(
                out=codes[:].bitcast(FP8X4), scales=scales[:], in_=woven[:].rearrange("p j i -> p (j i)")
            )
            h_quant[half, pair] = (codes, scales)

        def scores(acc, words, planes, block, passes):
            pair, first_mt = block // 2, 2 * (block % 2)
            for a in passes:
                codes, scales = h_quant[a, pair]
                for member in range(2):
                    cols = slice((first_mt + member) * P, (first_mt + member + 1) * P)
                    nc.tensor.matmul_mx(
                        out=acc[:, member, :],
                        lhsT=words[:, a, cols].bitcast(FP8X4), lhsT_scale=planes[:, a, cols],
                        rhs=codes[:].bitcast(FP8X4), rhs_scale=scales[:],
                        start=(a == 0 and member == 0), stop=(a == H_PASSES - 1 and member == 1),
                    )

        def load_w4_planes():
            planes = held([P, K_PASSES, H], U8, "w4_planes")
            nc.vector.memset(planes[:].bitcast(I32), 0)
            for quad in range(4):
                nc.sync.dma_start(
                    planes[32 * quad : 32 * quad + 4].bitcast(I32),
                    w4_scales.bitcast(I32)[:, 4 * quad : 4 * quad + 4, :].rearrange("a r c -> r a c"),
                )
            return planes

        w1_raw, w1_quant, neg_bent, squares, h_quant, tab_w = {}, {}, {}, {}, {}, {}
        sines = {}
        list1 = load_list(offs, "list1")
        tab_w[0] = load_words(tab_words, 0, 1, "tab_w0")
        tab_s = load_scale_rows(tab_scales, "tab_s", nc.sync)
        w4_codes = held([P, K_PASSES, 2 * H], U8, "w4_codes")
        nc.sync.dma_start(w4_codes[:].bitcast(I32), w4_words.bitcast(I32).rearrange("a p c -> p a c"))
        w4_planes = load_w4_planes()
        load_w1(0, 0)
        tab_w[1] = load_words(tab_words, 1, 1, "tab_w1")
        list2 = load_list(offs2, "list2")
        v_planes = gather_planes(tab_s, list1, K_PASSES, "v_planes", nc.sync)
        load_w1(0, 1)
        tab2_s = load_scale_rows(tab2_scales, "tab2_s", nc.sync)
        list3 = load_list(offs3, "list3")
        tab3_s = load_scale_rows(tab3_scales, "tab3_s", nc.sync)
        tab_w[2] = load_words(tab_words, 2, 1, "tab_w2")
        load_w1(0, 2)
        gain_tile = keep.tile([P, H_PASSES, PACK], F32, name="gain_tile")
        nc.sync.dma_start(gain_tile[:], gain.rearrange("(a p i) -> p a i", a=H_PASSES, i=PACK))
        v_words = {}
        for a in range(K_PASSES):
            v_words[a] = held([P, S], U32, "v_words%d" % a, "tab_s" if a == 0 else "")
            gather_words(v_words[a][:], tab_w[a][:, 0, :], list1)
        load_w1(1, 0)
        load_w1(1, 1)
        load_w1(1, 2)
        crew_picked = held([P, 2, S], U8, "crew_picked")
        nc.vector.tensor_copy(crew_picked[:, 0, :], tab2_s[:].indirect(list2[:]))
        nc.vector.tensor_copy(crew_picked[:, 1, :], tab3_s[:].indirect(list3[:]))
        crew_planes = held([P, H_PASSES, 2, S], U8, "crew_planes")
        nc.gpsimd.memset(crew_planes[:].bitcast(I32), 0)
        for quad in range(4):
            nc.sync.dma_start(
                crew_planes[32 * quad : 32 * quad + 4].rearrange("p a n s -> p a (n s)").bitcast(I32),
                crew_picked[8 * quad : 8 * (quad + 1)].rearrange("p n s -> p (n s)").bitcast(I32),
            )
        v2_planes, v3_planes = crew_planes[:, :, 0, :], crew_planes[:, :, 1, :]
        tab2_w = load_words(tab2_words, 0, H_PASSES, "tab2_w")
        tab3_w = load_words(tab3_words, 0, H_PASSES, "tab3_w")
        need_tile = held([P, M_TILES, S], F32, "need_tile")
        nc.sync.dma_start(need_tile[:], need.rearrange("(mt p) j -> p mt j", p=P))

        identity = held([P, P], F32, "identity")
        make_identity(nc, identity[:])
        one = keep.tile([P, 1], F32, name="one")
        nc.vector.memset(one[:], 1.0)
        minus_quarter_pi = keep.tile([P, 1], F32, name="minus_quarter_pi")
        nc.vector.tensor_scalar(minus_quarter_pi[:], one[:], -math.pi / 4, None, ALU.mult)
        table_choice = keep.tile([P, 1], F32, name="table_choice")
        nc.scalar.activation(table_choice[:], one[:], ACT.Silu)
        neg_gain = keep.tile([P, H_PASSES, PACK], F32, name="neg_gain")
        nc.gpsimd.tensor_scalar(neg_gain[:], gain_tile[:], -1.0, 0.0, ALU.mult, ALU.add)

        bent_acc = [bank(index, [P, PASS]) for index in range(H_PASSES * J_TILES)]
        quantize_w1(0, 0, [(512, 512, woven_tile(512, "woven0", "woven_a"))])
        for a in range(K_PASSES):
            for half in range(H_PASSES):
                for jt in range(J_TILES):
                    w4_pass(bent_acc[half * J_TILES + jt], half, jt, a)
        quantize_w1(0, 1, [(512, 512, woven_tile(512, "woven1", "woven_b"))])
        for half in range(H_PASSES):
            for jt in range(J_TILES):
                minus_tanh(bent_acc[half * J_TILES + jt], half, jt)
        quantize_w1(0, 2, [(512, 0, woven_tile(512, "woven2", "woven_a"))])
        for jt in range(J_TILES):
            acc = bank(jt, [P, PASS])
            for a in range(K_PASSES):
                w1_pass(acc, 0, jt, a)
            one_minus_sin(acc, 0, jt)
        quantize_w1(1, 0, [(512, 0, woven_tile(512, "woven3", "woven_b"))])
        quantize_w1(1, 1, [(512, 0, woven_tile(512, "woven4", "woven_a"))])
        quantize_w1(1, 2, [(512, 0, woven_tile(512, "woven5", "woven_b"))])
        wave_acc = [bank(J_TILES + jt, [P, PASS]) for jt in range(J_TILES)]
        for a in range(K_PASSES):
            for jt in range(J_TILES):
                w1_pass(wave_acc[jt], 1, jt, a)
        for jt in range(J_TILES):
            one_minus_sin(wave_acc[jt], 1, jt)
        for pair in range(J_TILES // 2):
            finish_h(0, pair)
        v2_words = held([P, H_PASSES, S], U32, "v2_words", "square03")
        for a in range(H_PASSES):
            gather_words(v2_words[:, a, :], tab2_w[:, a, :], list2)
        v3_words = held([P, H_PASSES, S], U32, "v3_words", "v_words2")
        for a in range(H_PASSES):
            gather_words(v3_words[:, a, :], tab3_w[:, a, :], list3)
        e2_acc = [bank(J_TILES + block, [P, 2, PAIR]) for block in range(J_TILES)]
        for block in range(J_TILES):
            scores(e2_acc[block], v2_words, v2_planes, block, (0,))
        for pair in range(J_TILES // 2):
            finish_h(1, pair)

        out_view = out.rearrange("(mt p) j -> p mt j", p=P)
        for block in range(J_TILES):
            e2 = e2_acc[block]
            e3 = bank(block, [P, 2, PAIR])
            scores(e2, v2_words, v2_planes, block, (1,))
            scores(e3, v3_words, v3_planes, block, (0, 1))
            rows = slice(2 * (block % 2), 2 * (block % 2) + 2)
            cols = slice(block // 2 * PAIR, (block // 2 + 1) * PAIR)
            bounded = ring.tile([P, 2, PAIR], F32, name="bounded")
            nc.scalar.activation(bounded[:], e2[:], ACT.Tanh)
            scaled = ring.tile([P, 2, PAIR], F32, name="scaled")
            nc.vector.tensor_tensor(scaled[:], bounded[:], need_tile[:, rows, cols], ALU.mult)
            result = ring.tile([P, 2, PAIR], F32, name="result")
            pieces = 2 if block == J_TILES - 1 else 1
            for piece in range(pieces):
                part = slice(piece * 2 // pieces, (piece + 1) * 2 // pieces)
                nc.vector.tensor_tensor(result[:, part, :], e3[:, part, :], scaled[:, part, :], ALU.add)
                nc.sync.dma_start(out_view[:, rows, cols][:, part, :], result[:, part, :])
